import numpy as np
import ml_dtypes


def mxq(x, axis, fmt="e4m3"):
    dtype, down = {"e4m3": (ml_dtypes.float8_e4m3fn, 7), "e5m2": (ml_dtypes.float8_e5m2, 14)}[fmt]
    v = np.moveaxis(np.asarray(x, np.float32).astype(ml_dtypes.bfloat16).astype(np.float64), axis, -1)
    blocks = v.reshape(v.shape[:-1] + (-1, 32))
    amax = np.abs(blocks).max(-1, keepdims=True)
    byte = np.maximum(np.where(amax > 0, np.frexp(amax)[1] - 1 + 127, 0) - down, 1)
    scale = np.exp2(byte - 127.0)
    codes = (blocks / scale).astype(np.float32).astype(dtype).astype(np.float64)
    return np.moveaxis((codes * scale).reshape(v.shape), -1, axis)


WIDE = False


def mx_kscale(k):
    if not WIDE:
        return np.ones(k)
    levels = np.array([10, -10, 5, -5, 0])
    if k % 512:
        return np.exp2(np.random.permutation(np.resize(levels, k // 32))).repeat(32)
    a = np.empty((k // 512, 16))
    for p in range(k // 512):
        a[p, :8] = np.random.permutation(np.resize(levels, 8))
        for g in range(8):
            far = levels[np.abs(levels - a[p, g]) >= 10]
            a[p, g + 8] = far[np.random.randint(len(far))]
    return np.exp2(a.ravel()).repeat(32)


def f64(x):
    return np.asarray(x).astype(np.float64)


def striped(idx):
    return np.tile(idx.reshape(-1, 16).T, (8, 1)).astype(np.uint16)


def unstriped(offs):
    return offs[:16].T.reshape(-1).astype(np.int64)


def striped8(idx):
    return np.concatenate([x.reshape(-1, 16).T for x in idx]).astype(np.uint16)


def runs(offs, k):
    lists = np.stack([offs[16 * r : 16 * r + 16].T.reshape(-1) for r in range(8)]).astype(np.int64)
    return lists[np.arange(k) % 512 // 64]


def pack_weight(w):
    k, n = w.shape
    w = f64(np.asarray(w, np.float32).astype(ml_dtypes.bfloat16)).reshape(k // 32, 32, n)
    amax = np.abs(w).max(1)
    byte = np.clip(np.where(amax > 0, np.frexp(amax)[1] - 1 + 127 - 7, 1), 1, 254)
    scaled = (w * np.exp2(127.0 - byte)[:, None, :]).reshape(k, n).astype(np.float32)
    words = np.ascontiguousarray(scaled.reshape(k // 512, 128, 4, n).transpose(0, 1, 3, 2)).astype(ml_dtypes.float8_e4m3fn).view(np.uint8)
    return words, np.ascontiguousarray(byte.astype(np.uint8).reshape(k // 512, 16, n))


def unpack_weight(words, scales):
    g, p, n, _ = words.shape
    vals = np.ascontiguousarray(words).view(ml_dtypes.float8_e4m3fn).astype(np.float64) * np.repeat(np.exp2(scales.astype(np.float64) - 127.0), 8, axis=1)[..., None]
    return vals.transpose(0, 1, 3, 2).reshape(g * 512, n)


K, T, S, N, H = 512, 2048, 512, 512, 512


def setup_inputs():
    n = np.random.standard_normal
    s = mx_kscale(K)[:, None]
    u = mx_kscale(H)
    packed_xT = pack_weight(n((K, T)) * s)
    return {
        "x_words": packed_xT[0],
        "x_scales": packed_xT[1],
        "w1": (n((K, H)) / np.sqrt(K) / s).astype(np.float32),
        "w2": (n((K, H)) / np.sqrt(K) / s).astype(np.float32),
        "a1": np.random.uniform(0.2, 0.8, (H, S)).astype(np.float32),
        "a2": np.random.uniform(0.2, 0.8, (H, S)).astype(np.float32),
        "gn": (np.random.uniform(0.5, 1.5, (H, 1)) * u[:, None]).astype(np.float32),
        "w3": (n((H, N)) / np.sqrt(H) / u[:, None]).astype(np.float32),
        "offs": striped(np.random.permutation(T)[:S]),
        "ref": striped(np.random.permutation(T)[:S]),
        "c1": striped8(np.stack([np.random.permutation(S) for _ in range(8)])),
        "c2": striped8(np.stack([np.random.permutation(S) for _ in range(8)])),
    }


def reference(x_words, x_scales, w1, w2, a1, a2, gn, w3, offs, ref, c1, c2):
    xq = unpack_weight(x_words, x_scales)[:, unstriped(offs)]
    y = mxq(f64(w1), 0, "e4m3").T @ xq
    x_ref = unpack_weight(x_words, x_scales)[:, unstriped(ref)]
    e = mxq(f64(w2), 0, "e4m3").T @ x_ref
    z = f64(gn) * (np.clip(y - (f64(a1) * (e[np.arange(H)[:, None], runs(c1, H)]) + f64(a2) * (e[np.arange(H)[:, None], runs(c2, H)])), -1.5, 1.5))
    return mxq(f64(w3), 0, "e4m3").T @ mxq(z, 0, "e4m3")

@@ -1,0 +1,214 @@
+from contextlib import ExitStack
+
+import concourse.mybir as mybir
+
+F32 = mybir.dt.float32
+BF16 = mybir.dt.bfloat16
+I32 = mybir.dt.int32
+U32 = mybir.dt.uint32
+U16 = mybir.dt.uint16
+U8 = mybir.dt.uint8
+FP8X4 = mybir.dt.float8_e4m3fn_x4
+ALU = mybir.AluOpType
+ACT = mybir.ActivationFunctionType
+
+P = 128
+PACK = 4
+T, S, H, N = 2048, 512, 512, 512
+CLIP = 1.5
+FLOPS = 3 * 2 * 512 * 512 * 512
+CHUNKS = ((0, 384), (384, 512))
+
+
+def pieces(lo, hi):
+    runs = []
+    while lo < hi:
+        width = 256 if hi - lo >= 256 else 128
+        runs.append((lo, lo + width))
+        lo = lo + width
+    return runs
+
+
+def tile_picked_mcresid_none_p_kernel(
+    tc, x_words, x_scales, w1, w2, a1, a2, gn, w3, offs, ref, c1, c2, out
+):
+    nc = tc.nc
+    with ExitStack() as ctx:
+        lists = ctx.enter_context(tc.tile_pool(name="lists", bufs=1))
+        keep = ctx.enter_context(tc.tile_pool(name="keep", bufs=1))
+        work = ctx.enter_context(tc.tile_pool(name="work", bufs=2))
+        psum = ctx.enter_context(tc.psum_pool(name="psum", bufs=1))
+
+        def load_list(name, src):
+            tile = lists.tile([P, S // 16], U16, name=name)
+            nc.sync.dma_start(tile[:], src)
+            return tile
+
+        def load_weight(name, src):
+            raw = keep.tile([P, PACK, 512], F32, name=name)
+            nc.sync.dma_start(raw[:], src.rearrange("(p j) c -> p j c", j=PACK))
+            return raw
+
+        def load_rows(name, src, t):
+            tile = keep.tile([P, S], F32, name=name)
+            nc.sync.dma_start(tile[:], src.rearrange("(p t) c -> t p c", t=PACK)[t])
+            return tile
+
+        x_bytes = keep.tile([P, T], U8, name="x_bytes", align_bytes=64)
+        nc.vector.memset(x_bytes[:].bitcast(I32), 0)
+        ref_list = load_list("ref_list", ref)
+        w2_view = w2.rearrange("(p j) c -> p j c", j=PACK)
+        w2_halves = [keep.tile([P, PACK, 256], F32, name="w2_raw%d" % h) for h in range(2)]
+        nc.sync.dma_start(w2_halves[0][:], w2_view[:, :, 0:256])
+        for r in range(4):
+            nc.sync.dma_start(
+                x_bytes[r:P:32, :].bitcast(I32),
+                x_scales[0].rearrange("(q r) c -> r q c", r=4)[r].bitcast(I32),
+            )
+        offs_list = load_list("offs_list", offs)
+        nc.sync.dma_start(w2_halves[1][:], w2_view[:, :, 256:512])
+        x_packed = keep.tile([P, T], I32, name="x_packed", align_bytes=64)
+        nc.sync.dma_start(x_packed[:], x_words[0].rearrange("p c r -> p (c r)").bitcast(I32))
+        gain = keep.tile([P, PACK], F32, name="gain")
+        nc.sync.dma_start(gain[:], gn.rearrange("(p t) o -> p (t o)", t=PACK))
+        c1_list = load_list("c1_list", c1)
+        c2_list = load_list("c2_list", c2)
+        a_rows = {}
+        for t in (0, 1):
+            a_rows[0, t] = load_rows("a1_%d" % t, a1, t)
+            a_rows[1, t] = load_rows("a2_%d" % t, a2, t)
+        w1_raw = load_weight("w1_raw", w1)
+        for t in (2, 3):
+            a_rows[0, t] = load_rows("a1_%d" % t, a1, t)
+            a_rows[1, t] = load_rows("a2_%d" % t, a2, t)
+        w3_raw = load_weight("w3_raw", w3)
+
+        def gather_bytes(name, picks):
+            tile = keep.tile([P, S], U8, name=name, align_bytes=64)
+            nc.vector.tensor_copy(tile[:], x_bytes[:].indirect(picks[:]))
+            return tile
+
+        def gather_words(name, picks):
+            tile = keep.tile([P, S], U32, name=name, align_bytes=64)
+            nc.vector.tensor_copy(tile[:], x_packed[:].bitcast(U32).indirect(picks[:]))
+            return tile
+
+        def round_dealt(name, raw, copy):
+            grouped = keep.tile([P, 512 * PACK], BF16, name=name, align_bytes=64)
+            copy(
+                grouped[:].rearrange("p (t m j) -> p m j t", t=PACK, j=PACK),
+                raw[:].rearrange("p j (m t) -> p m j t", t=PACK),
+            )
+            return grouped
+
+        def round_plain(name, raw, copy):
+            grouped = keep.tile([P, 512 * PACK], BF16, name=name, align_bytes=64)
+            copy(
+                grouped[:].rearrange("p (c i j) -> p c j i", i=4, j=PACK),
+                raw[:].rearrange("p j (c i) -> p c j i", i=4),
+            )
+            return grouped
+
+        def quantise(name, grouped, width, pool):
+            codes = pool.tile([P, width], U32, name=name + "_codes", align_bytes=64)
+            scales = pool.tile([P, width], U8, name=name + "_scales", align_bytes=64)
+            nc.vector.quantize_mx(out=codes[:].bitcast(FP8X4), scales=scales[:], in_=grouped)
+            return codes, scales
+
+        def product(bank, stationary, block, moving):
+            cols = slice(block * P, (block + 1) * P)
+            nc.tensor.matmul_mx(
+                out=bank,
+                lhsT=stationary[0][:, cols].bitcast(FP8X4),
+                lhsT_scale=stationary[1][:, cols],
+                rhs=moving[0][:].bitcast(FP8X4),
+                rhs_scale=moving[1][:],
+                start=True,
+                stop=True,
+            )
+
+        ref_bytes = gather_bytes("ref_bytes", ref_list)
+        offs_bytes = gather_bytes("offs_bytes", offs_list)
+        w2_grouped = keep.tile([P, 512 * PACK], BF16, name="w2_grouped", align_bytes=64)
+        for h in range(2):
+            nc.scalar.copy(
+                w2_grouped[:].rearrange("p (t m j) -> p m j t", t=PACK, j=PACK)[:, 64 * h : 64 * (h + 1)],
+                w2_halves[h][:].rearrange("p j (m t) -> p m j t", t=PACK),
+            )
+        w2_q = quantise("w2", w2_grouped[:], 512, keep)
+        ref_words = gather_words("ref_words", ref_list)
+        offs_words = gather_words("offs_words", offs_list)
+
+        e_rows = []
+        for t in range(PACK):
+            bank = psum.tile([P, S], F32, name="e_bank%d" % t, tag="late%d" % t)
+            product(bank[:], w2_q, t, (ref_words, ref_bytes))
+            row = keep.tile([P, S], F32, name="e_row%d" % t)
+            nc.scalar.activation(row[:], bank[:], ACT.Copy, scale=gain[:, t : t + 1])
+            e_rows.append(row)
+
+        upper = keep.tile([P, PACK], F32, name="upper")
+        lower = keep.tile([P, PACK], F32, name="lower")
+        nc.scalar.activation(upper[:], gain[:], ACT.Abs, scale=CLIP)
+        nc.scalar.activation(lower[:], upper[:], ACT.Copy, scale=-1.0)
+
+        w1_grouped = round_dealt("w1_grouped", w1_raw, nc.scalar.copy)
+        w3_grouped = round_plain("w3_grouped", w3_raw, nc.scalar.copy)
+
+        y_banks = []
+        quantised = {}
+        out_rows = out.rearrange("(b p) j -> p b j", p=P)
+        for lo, hi in CHUNKS:
+            width = hi - lo
+            z_planes = keep.tile([P, PACK, width], BF16, name="z_planes%d" % lo, align_bytes=64)
+            predicted = []
+            for t in range(PACK):
+                terms = []
+                for side, picks in enumerate((c1_list, c2_list)):
+                    term = work.tile([P, width], F32, name="term%d_%d" % (side, lo))
+                    nc.vector.tensor_tensor(
+                        term[:],
+                        e_rows[t][:].indirect(picks[:, lo // 16 : hi // 16]),
+                        a_rows[side, t][:, lo:hi],
+                        ALU.mult,
+                    )
+                    terms.append(term)
+                both = keep.tile([P, width], F32, name="both%d_%d" % (t, lo))
+                nc.vector.tensor_tensor(both[:], terms[0][:], terms[1][:], ALU.add)
+                predicted.append(both)
+                if lo == 0 and t == 2:
+                    quantised["w1"] = quantise("w1", w1_grouped[:], 512, keep)
+                    for u in range(PACK):
+                        bank = psum.tile([P, S], F32, name="y_bank%d" % u)
+                        product(bank[:], quantised["w1"], u, (offs_words, offs_bytes))
+                        y_banks.append(bank)
+            residuals = []
+            for t in range(PACK):
+                residual = keep.tile([P, width], F32, name="residual%d_%d" % (t, lo))
+                nc.vector.scalar_tensor_tensor(
+                    residual[:], y_banks[t][:, lo:hi], gain[:, t : t + 1], predicted[t][:], ALU.mult, ALU.subtract
+                )
+                residuals.append(residual)
+            for t in range(PACK):
+                nc.vector.tensor_scalar(
+                    z_planes[:, t, :], residuals[t][:], lower[:, t : t + 1], upper[:, t : t + 1], ALU.max, ALU.min
+                )
+            if lo == 0:
+                quantised["w3"] = quantise("w3", w3_grouped[:], 512, keep)
+            weave = nc.scalar.copy if lo == 0 else nc.vector.tensor_copy
+            for a, b in pieces(lo, hi):
+                z_grouped = keep.tile([P, (b - a) * PACK], BF16, name="z_grouped%d" % a, align_bytes=64)
+                weave(
+                    z_grouped[:].rearrange("p (c i t) -> p c t i", i=4, t=PACK),
+                    z_planes[:, :, a - lo : b - lo].rearrange("p t (c i) -> p c t i", i=4),
+                )
+                z_q = quantise("z%d" % a, z_grouped[:], b - a, keep)
+                per_bank = S // (b - a) // 2 if lo else S // (b - a)
+                staged = keep.tile([P, PACK, b - a], F32, name="staged%d" % a)
+                for g in range(PACK // per_bank):
+                    bank = psum.tile([P, per_bank, b - a], F32, name="out_bank%d_%d" % (a, g), tag="late%d" % ((g + a // 128) % PACK))
+                    for i in range(per_bank):
+                        product(bank[:, i, :], quantised["w3"], g * per_bank + i, z_q)
+                    copy = nc.vector.tensor_copy if lo and g == 1 else nc.scalar.copy
+                    copy(staged[:, g * per_bank : (g + 1) * per_bank, :], bank[:])
+                nc.sync.dma_start(out_rows[:, :, a:b], staged[:])

@@ -1,6 +1,7 @@
 from contextlib import ExitStack
 
 import concourse.mybir as mybir
+from concourse.masks import make_identity
 
 F32 = mybir.dt.float32
 BF16 = mybir.dt.bfloat16
@@ -17,16 +18,8 @@ PACK = 4
 T, S, H, N = 2048, 512, 512, 512
 CLIP = 1.5
 FLOPS = 3 * 2 * 512 * 512 * 512
-CHUNKS = ((0, 384), (384, 512))
-
-
-def pieces(lo, hi):
-    runs = []
-    while lo < hi:
-        width = 256 if hi - lo >= 256 else 128
-        runs.append((lo, lo + width))
-        lo = lo + width
-    return runs
+HALF = 256
+BLOCKS = 4
 
 
 def tile_picked_mcresid_none_p_kernel(
@@ -36,7 +29,6 @@ def tile_picked_mcresid_none_p_kernel(
     with ExitStack() as ctx:
         lists = ctx.enter_context(tc.tile_pool(name="lists", bufs=1))
         keep = ctx.enter_context(tc.tile_pool(name="keep", bufs=1))
-        work = ctx.enter_context(tc.tile_pool(name="work", bufs=2))
         psum = ctx.enter_context(tc.psum_pool(name="psum", bufs=1))
 
         def load_list(name, src):
@@ -49,9 +41,9 @@ def tile_picked_mcresid_none_p_kernel(
             nc.sync.dma_start(raw[:], src.rearrange("(p j) c -> p j c", j=PACK))
             return raw
 
-        def load_rows(name, src, t):
-            tile = keep.tile([P, S], F32, name=name)
-            nc.sync.dma_start(tile[:], src.rearrange("(p t) c -> t p c", t=PACK)[t])
+        def load_half(name, src, h):
+            tile = keep.tile([P, PACK, HALF], F32, name=name)
+            nc.sync.dma_start(tile[:], src.rearrange("(p t) c -> p t c", t=PACK)[:, :, h * HALF : (h + 1) * HALF])
             return tile
 
         x_bytes = keep.tile([P, T], U8, name="x_bytes", align_bytes=64)
@@ -73,14 +65,12 @@ def tile_picked_mcresid_none_p_kernel(
         nc.sync.dma_start(gain[:], gn.rearrange("(p t) o -> p (t o)", t=PACK))
         c1_list = load_list("c1_list", c1)
         c2_list = load_list("c2_list", c2)
-        a_rows = {}
-        for t in (0, 1):
-            a_rows[0, t] = load_rows("a1_%d" % t, a1, t)
-            a_rows[1, t] = load_rows("a2_%d" % t, a2, t)
+        a_half = {}
+        a_half[0, 0] = load_half("a1_0", a1, 0)
         w1_raw = load_weight("w1_raw", w1)
-        for t in (2, 3):
-            a_rows[0, t] = load_rows("a1_%d" % t, a1, t)
-            a_rows[1, t] = load_rows("a2_%d" % t, a2, t)
+        a_half[1, 0] = load_half("a2_0", a2, 0)
+        a_half[0, 1] = load_half("a1_1", a1, 1)
+        a_half[1, 1] = load_half("a2_1", a2, 1)
         w3_raw = load_weight("w3_raw", w3)
 
         def gather_bytes(name, picks):
@@ -88,9 +78,12 @@ def tile_picked_mcresid_none_p_kernel(
             nc.vector.tensor_copy(tile[:], x_bytes[:].indirect(picks[:]))
             return tile
 
-        def gather_words(name, picks):
+        def gather_words(name, picks, parts):
             tile = keep.tile([P, S], U32, name=name, align_bytes=64)
-            nc.vector.tensor_copy(tile[:], x_packed[:].bitcast(U32).indirect(picks[:]))
+            width = S // parts
+            for i in range(parts):
+                entries = picks[:, i * width // 16 : (i + 1) * width // 16]
+                nc.vector.tensor_copy(tile[:, i * width : (i + 1) * width], x_packed[:].bitcast(U32).indirect(entries))
             return tile
 
         def round_dealt(name, raw, copy):
@@ -109,20 +102,20 @@ def tile_picked_mcresid_none_p_kernel(
             )
             return grouped
 
-        def quantise(name, grouped, width, pool):
-            codes = pool.tile([P, width], U32, name=name + "_codes", align_bytes=64)
+        def quantise(name, grouped, width, pool, tag=None):
+            codes = pool.tile([P, width], U32, name=name + "_codes", tag=tag or name + "_codes", align_bytes=64)
             scales = pool.tile([P, width], U8, name=name + "_scales", align_bytes=64)
             nc.vector.quantize_mx(out=codes[:].bitcast(FP8X4), scales=scales[:], in_=grouped)
             return codes, scales
 
-        def product(bank, stationary, block, moving):
+        def product(bank, stationary, block, moving, lo, hi):
             cols = slice(block * P, (block + 1) * P)
             nc.tensor.matmul_mx(
                 out=bank,
                 lhsT=stationary[0][:, cols].bitcast(FP8X4),
                 lhsT_scale=stationary[1][:, cols],
-                rhs=moving[0][:].bitcast(FP8X4),
-                rhs_scale=moving[1][:],
+                rhs=moving[0][:, lo:hi].bitcast(FP8X4),
+                rhs_scale=moving[1][:, lo:hi],
                 start=True,
                 stop=True,
             )
@@ -136,79 +129,109 @@ def tile_picked_mcresid_none_p_kernel(
                 w2_halves[h][:].rearrange("p j (m t) -> p m j t", t=PACK),
             )
         w2_q = quantise("w2", w2_grouped[:], 512, keep)
-        ref_words = gather_words("ref_words", ref_list)
-        offs_words = gather_words("offs_words", offs_list)
+        ref_words = gather_words("ref_words", ref_list, 2)
+        offs_words = gather_words("offs_words", offs_list, 1)
+
+        identity = keep.tile([P, P], F32, name="identity")
+        make_identity(nc, identity[:])
 
         e_rows = []
         for t in range(PACK):
-            bank = psum.tile([P, S], F32, name="e_bank%d" % t, tag="late%d" % t)
-            product(bank[:], w2_q, t, (ref_words, ref_bytes))
-            row = keep.tile([P, S], F32, name="e_row%d" % t)
-            nc.scalar.activation(row[:], bank[:], ACT.Copy, scale=gain[:, t : t + 1])
+            row = keep.tile([P, S], F32, name="e_row%d" % t, align_bytes=64)
+            spans = ((0, HALF, "block0"), (HALF, S, "plane0")) if t == 0 else ((0, S, "plane%d" % t),)
+            for lo, hi, tag in spans:
+                bank = psum.tile([P, hi - lo], F32, name="e_bank%d_%d" % (t, lo), tag=tag)
+                product(bank[:], w2_q, t, (ref_words, ref_bytes), lo, hi)
+                nc.scalar.activation(row[:, lo:hi], bank[:], ACT.Copy, scale=-1.0)
             e_rows.append(row)
 
-        upper = keep.tile([P, PACK], F32, name="upper")
-        lower = keep.tile([P, PACK], F32, name="lower")
-        nc.scalar.activation(upper[:], gain[:], ACT.Abs, scale=CLIP)
-        nc.scalar.activation(lower[:], upper[:], ACT.Copy, scale=-1.0)
-
         w1_grouped = round_dealt("w1_grouped", w1_raw, nc.scalar.copy)
-        w3_grouped = round_plain("w3_grouped", w3_raw, nc.scalar.copy)
 
-        y_banks = []
-        quantised = {}
-        out_rows = out.rearrange("(b p) j -> p b j", p=P)
-        for lo, hi in CHUNKS:
-            width = hi - lo
-            z_planes = keep.tile([P, PACK, width], BF16, name="z_planes%d" % lo, align_bytes=64)
-            predicted = []
-            for t in range(PACK):
-                terms = []
-                for side, picks in enumerate((c1_list, c2_list)):
-                    term = work.tile([P, width], F32, name="term%d_%d" % (side, lo))
-                    nc.vector.tensor_tensor(
-                        term[:],
-                        e_rows[t][:].indirect(picks[:, lo // 16 : hi // 16]),
-                        a_rows[side, t][:, lo:hi],
-                        ALU.mult,
+        sums = [psum.tile([P, PACK, P], F32, name="sums%d" % b, tag="block%d" % b) for b in range(BLOCKS)]
+
+        def add_turned(src, t, b, start, stop):
+            nc.tensor.matmul(sums[b][:, t, :], lhsT=src, rhs=identity[:], start=start, stop=stop, is_transpose=True)
+
+        def predict(side, h, planes, tag, closes):
+            picks = (c1_list, c2_list)[side]
+            terms = keep.tile([P, len(planes), HALF], F32, name="terms%d_%d_%d" % (side, h, planes[0]), tag=tag, align_bytes=64)
+            for n, t in enumerate(planes):
+                nc.vector.tensor_tensor(
+                    terms[:, n, :],
+                    e_rows[t][:].indirect(picks[:, h * HALF // 16 : (h + 1) * HALF // 16]),
+                    a_half[side, h][:, t, :],
+                    ALU.mult,
+                )
+                for i in range(2):
+                    add_turned(
+                        terms[:, n, i * P : (i + 1) * P], t, 2 * h + i, t == 0 and side == 0, closes and t == PACK - 1
                     )
-                    terms.append(term)
-                both = keep.tile([P, width], F32, name="both%d_%d" % (t, lo))
-                nc.vector.tensor_tensor(both[:], terms[0][:], terms[1][:], ALU.add)
-                predicted.append(both)
-                if lo == 0 and t == 2:
-                    quantised["w1"] = quantise("w1", w1_grouped[:], 512, keep)
-                    for u in range(PACK):
-                        bank = psum.tile([P, S], F32, name="y_bank%d" % u)
-                        product(bank[:], quantised["w1"], u, (offs_words, offs_bytes))
-                        y_banks.append(bank)
-            residuals = []
+
+        def clip(b):
+            clipped = keep.tile([P, PACK, P], F32, name="clipped%d" % b)
+            nc.vector.tensor_scalar(clipped[:], sums[b][:], -CLIP, CLIP, ALU.max, ALU.min)
+            return clipped
+
+        out_rows = out.rearrange("(b p) j -> p b j", p=P)
+
+        def finish(z_grouped, lo, hi, tags, copies):
+            z_q = quantise("z%d" % lo, z_grouped[:].rearrange("p j t -> p (j t)"), hi - lo, keep)
+            staged = keep.tile([P, PACK, hi - lo], F32, name="staged%d" % lo)
+            for g in range(2):
+                bank = psum.tile([P, 2, hi - lo], F32, name="out_bank%d_%d" % (lo, g), tag=tags[g])
+                for i in range(2):
+                    product(bank[:, i, :], w3_q, 2 * g + i, z_q, 0, hi - lo)
+                copies[g](staged[:, 2 * g : 2 * g + 2, :], bank[:])
+            nc.sync.dma_start(out_rows[:, :, lo:hi], staged[:])
+
+        planes = tuple(range(PACK))
+        predict(0, 0, planes, "terms00", False)
+        predict(1, 0, planes, "terms10", False)
+        w1_q = quantise("w1", w1_grouped[:], 512, keep)
+        y_rows = []
+        for t in range(PACK):
+            bank = psum.tile([P, S], F32, name="y_bank%d" % t, tag="plane%d" % t)
+            product(bank[:], w1_q, t, (offs_words, offs_bytes), 0, S)
+            row = keep.tile([P, S], F32, name="y_row%d" % t, align_bytes=64)
+            nc.scalar.copy(row[:], bank[:])
+            y_rows.append(row)
+        w3_grouped = round_plain("w3_grouped", w3_raw, nc.scalar.copy)
+        predict(0, 1, planes, "w1_grouped", False)
+        for t in range(PACK):
+            for b in range(BLOCKS):
+                add_turned(y_rows[t][:, b * P : (b + 1) * P], t, b, False, b < 2 and t == PACK - 1)
+        predict(1, 1, planes[:3], "terms11", False)
+
+        first = [clip(b) for b in range(2)]
+        z_planes = keep.tile([P, PACK, HALF], BF16, name="z_planes", align_bytes=64)
+        for t in range(PACK):
+            bank = psum.tile([P, HALF], F32, name="back_plane%d" % t, tag="plane%d" % t)
+            for b in range(2):
+                nc.tensor.transpose(bank[:, b * P : (b + 1) * P], first[b][:, t, :], identity[:])
+            nc.scalar.activation(z_planes[:, t, :], bank[:], ACT.Copy, scale=gain[:, t : t + 1])
+        z_first = keep.tile([P, HALF, PACK], BF16, name="z_first", align_bytes=64)
+        nc.scalar.copy(
+            z_first[:].rearrange("p (c i) t -> p c t i", i=4), z_planes[:].rearrange("p t (c i) -> p c t i", i=4)
+        )
+
+        predict(1, 1, planes[3:], "y_row3", True)
+        w3_q = quantise("w3", w3_grouped[:], 512, keep, "e_row3")
+        backs = []
+        for b in (2, 3):
+            clipped = clip(b)
+            bank = psum.tile([P, PACK, P], F32, name="back_block%d" % b, tag="block%d" % (b - 2))
             for t in range(PACK):
-                residual = keep.tile([P, width], F32, name="residual%d_%d" % (t, lo))
-                nc.vector.scalar_tensor_tensor(
-                    residual[:], y_banks[t][:, lo:hi], gain[:, t : t + 1], predicted[t][:], ALU.mult, ALU.subtract
-                )
-                residuals.append(residual)
-            for t in range(PACK):
-                nc.vector.tensor_scalar(
-                    z_planes[:, t, :], residuals[t][:], lower[:, t : t + 1], upper[:, t : t + 1], ALU.max, ALU.min
-                )
-            if lo == 0:
-                quantised["w3"] = quantise("w3", w3_grouped[:], 512, keep)
-            weave = nc.scalar.copy if lo == 0 else nc.vector.tensor_copy
-            for a, b in pieces(lo, hi):
-                z_grouped = keep.tile([P, (b - a) * PACK], BF16, name="z_grouped%d" % a, align_bytes=64)
-                weave(
-                    z_grouped[:].rearrange("p (c i t) -> p c t i", i=4, t=PACK),
-                    z_planes[:, :, a - lo : b - lo].rearrange("p t (c i) -> p c t i", i=4),
-                )
-                z_q = quantise("z%d" % a, z_grouped[:], b - a, keep)
-                per_bank = S // (b - a) // 2 if lo else S // (b - a)
-                staged = keep.tile([P, PACK, b - a], F32, name="staged%d" % a)
-                for g in range(PACK // per_bank):
-                    bank = psum.tile([P, per_bank, b - a], F32, name="out_bank%d_%d" % (a, g), tag="late%d" % ((g + a // 128) % PACK))
-                    for i in range(per_bank):
-                        product(bank[:, i, :], quantised["w3"], g * per_bank + i, z_q)
-                    copy = nc.vector.tensor_copy if lo and g == 1 else nc.scalar.copy
-                    copy(staged[:, g * per_bank : (g + 1) * per_bank, :], bank[:])
-                nc.sync.dma_start(out_rows[:, :, a:b], staged[:])
+                nc.tensor.transpose(bank[:, t, :], clipped[:, t, :], identity[:])
+            backs.append(bank)
+        finish(z_first, 0, HALF, ("plane0", "plane1"), (nc.scalar.copy, nc.scalar.copy))
+
+        gain_wide = gain[:].unsqueeze(1).to_broadcast([P, P, PACK])
+        z_last = []
+        for b in (2, 3):
+            z_grouped = keep.tile([P, P, PACK], BF16, name="z_grouped%d" % b, tag="z_first" if b == 2 else "z_last", align_bytes=64)
+            nc.vector.tensor_tensor(z_grouped[:], backs[b - 2][:].rearrange("p t j -> p j t"), gain_wide, ALU.mult)
+            z_last.append(z_grouped)
+        for b in (2, 3):
+            finish(
+                z_last[b - 2], b * P, (b + 1) * P, ("block%d" % b, "plane%d" % b), (nc.scalar.copy, nc.vector.tensor_copy)
+            )

@@ -42,7 +42,7 @@ def tile_picked_mcresid_none_p_kernel(
             return raw
 
         def load_half(name, src, h):
-            tile = keep.tile([P, PACK, HALF], F32, name=name)
+            tile = keep.tile([P, PACK, HALF], F32, name=name, align_bytes=64)
             nc.sync.dma_start(tile[:], src.rearrange("(p t) c -> p t c", t=PACK)[:, :, h * HALF : (h + 1) * HALF])
             return tile
 
@@ -69,9 +69,10 @@ def tile_picked_mcresid_none_p_kernel(
         a_half[0, 0] = load_half("a1_0", a1, 0)
         w1_raw = load_weight("w1_raw", w1)
         a_half[1, 0] = load_half("a2_0", a2, 0)
+        w3_halves = [load_half("w3_0", w3, 0)]
         a_half[0, 1] = load_half("a1_1", a1, 1)
         a_half[1, 1] = load_half("a2_1", a2, 1)
-        w3_raw = load_weight("w3_raw", w3)
+        w3_halves.append(load_half("w3_1", w3, 1))
 
         def gather_bytes(name, picks):
             tile = keep.tile([P, S], U8, name=name, align_bytes=64)
@@ -94,13 +95,11 @@ def tile_picked_mcresid_none_p_kernel(
             )
             return grouped
 
-        def round_plain(name, raw, copy):
-            grouped = keep.tile([P, 512 * PACK], BF16, name=name, align_bytes=64)
-            copy(
-                grouped[:].rearrange("p (c i j) -> p c j i", i=4, j=PACK),
+        def round_plain(grouped, raw):
+            nc.scalar.copy(
+                grouped.rearrange("p (c i j) -> p c j i", i=4, j=PACK),
                 raw[:].rearrange("p j (c i) -> p c j i", i=4),
             )
-            return grouped
 
         def quantise(name, grouped, width, pool, tag=None):
             codes = pool.tile([P, width], U32, name=name + "_codes", tag=tag or name + "_codes", align_bytes=64)
@@ -146,15 +145,19 @@ def tile_picked_mcresid_none_p_kernel(
             e_rows.append(row)
 
         w1_grouped = round_dealt("w1_grouped", w1_raw, nc.scalar.copy)
+        w3_grouped = keep.tile([P, 512 * PACK], BF16, name="w3_grouped", align_bytes=64)
+        round_plain(w3_grouped[:, 0 : HALF * PACK], w3_halves[0])
 
         sums = [psum.tile([P, PACK, P], F32, name="sums%d" % b, tag="block%d" % b) for b in range(BLOCKS)]
 
         def add_turned(src, t, b, start, stop):
             nc.tensor.matmul(sums[b][:, t, :], lhsT=src, rhs=identity[:], start=start, stop=stop, is_transpose=True)
 
-        def predict(side, h, planes, tag, closes):
+        def term_tile(count, tag):
+            return keep.tile([P, count, HALF], F32, name="terms_" + tag, tag=tag, align_bytes=64)
+
+        def predict(side, h, planes, terms, closes):
             picks = (c1_list, c2_list)[side]
-            terms = keep.tile([P, len(planes), HALF], F32, name="terms%d_%d_%d" % (side, h, planes[0]), tag=tag, align_bytes=64)
             for n, t in enumerate(planes):
                 nc.vector.tensor_tensor(
                     terms[:, n, :],
@@ -164,7 +167,7 @@ def tile_picked_mcresid_none_p_kernel(
                 )
                 for i in range(2):
                     add_turned(
-                        terms[:, n, i * P : (i + 1) * P], t, 2 * h + i, t == 0 and side == 0, closes and t == PACK - 1
+                        terms[:, n, i * P : (i + 1) * P], t, 2 * h + i, t == 0 and side == 0 and h == 0, closes and t == PACK - 1
                     )
 
         def clip(b):
@@ -174,7 +177,7 @@ def tile_picked_mcresid_none_p_kernel(
 
         out_rows = out.rearrange("(b p) j -> p b j", p=P)
 
-        def finish(z_grouped, lo, hi, tags, copies):
+        def finish(z_grouped, lo, hi, tags, copies, stores):
             z_q = quantise("z%d" % lo, z_grouped[:].rearrange("p j t -> p (j t)"), hi - lo, keep)
             staged = keep.tile([P, PACK, hi - lo], F32, name="staged%d" % lo)
             for g in range(2):
@@ -182,25 +185,29 @@ def tile_picked_mcresid_none_p_kernel(
                 for i in range(2):
                     product(bank[:, i, :], w3_q, 2 * g + i, z_q, 0, hi - lo)
                 copies[g](staged[:, 2 * g : 2 * g + 2, :], bank[:])
-            nc.sync.dma_start(out_rows[:, :, lo:hi], staged[:])
+            for g in range(stores):
+                rows = slice(g * PACK // stores, (g + 1) * PACK // stores)
+                nc.sync.dma_start(out_rows[:, rows, lo:hi], staged[:, rows, :])
 
         planes = tuple(range(PACK))
-        predict(0, 0, planes, "terms00", False)
-        predict(1, 0, planes, "terms10", False)
+        predict(0, 0, planes, term_tile(4, "first"), False)
+        predict(1, 0, planes[:3], term_tile(3, "second"), False)
         w1_q = quantise("w1", w1_grouped[:], 512, keep)
-        y_rows = []
+        y_banks = []
         for t in range(PACK):
             bank = psum.tile([P, S], F32, name="y_bank%d" % t, tag="plane%d" % t)
             product(bank[:], w1_q, t, (offs_words, offs_bytes), 0, S)
-            row = keep.tile([P, S], F32, name="y_row%d" % t, align_bytes=64)
-            nc.scalar.copy(row[:], bank[:])
-            y_rows.append(row)
-        w3_grouped = round_plain("w3_grouped", w3_raw, nc.scalar.copy)
-        predict(0, 1, planes, "w1_grouped", False)
-        for t in range(PACK):
-            for b in range(BLOCKS):
-                add_turned(y_rows[t][:, b * P : (b + 1) * P], t, b, False, b < 2 and t == PACK - 1)
-        predict(1, 1, planes[:3], "terms11", False)
+            y_banks.append(bank)
+        after_w1 = term_tile(5, "w1_grouped")
+        predict(1, 0, planes[3:], after_w1[:, 0:1, :], False)
+        for h in range(2):
+            y_half = keep.tile([P, PACK, HALF], F32, name="y_half%d" % h, tag=("w3_0", "y_last")[h], align_bytes=64)
+            for t in range(PACK):
+                nc.scalar.copy(y_half[:, t, :], y_banks[t][:, h * HALF : (h + 1) * HALF])
+                for i in range(2):
+                    add_turned(y_half[:, t, i * P : (i + 1) * P], t, 2 * h + i, h == 1 and t == 0, h == 0 and t == PACK - 1)
+        round_plain(w3_grouped[:, HALF * PACK :], w3_halves[1])
+        predict(0, 1, planes, after_w1[:, 1:5, :], False)
 
         first = [clip(b) for b in range(2)]
         z_planes = keep.tile([P, PACK, HALF], BF16, name="z_planes", align_bytes=64)
@@ -214,7 +221,7 @@ def tile_picked_mcresid_none_p_kernel(
             z_first[:].rearrange("p (c i) t -> p c t i", i=4), z_planes[:].rearrange("p t (c i) -> p c t i", i=4)
         )
 
-        predict(1, 1, planes[3:], "y_row3", True)
+        predict(1, 1, planes, term_tile(4, "w3_0"), True)
         w3_q = quantise("w3", w3_grouped[:], 512, keep, "e_row3")
         backs = []
         for b in (2, 3):
@@ -223,7 +230,7 @@ def tile_picked_mcresid_none_p_kernel(
             for t in range(PACK):
                 nc.tensor.transpose(bank[:, t, :], clipped[:, t, :], identity[:])
             backs.append(bank)
-        finish(z_first, 0, HALF, ("plane0", "plane1"), (nc.scalar.copy, nc.scalar.copy))
+        finish(z_first, 0, HALF, ("plane0", "plane1"), (nc.scalar.copy, nc.scalar.copy), 2)
 
         gain_wide = gain[:].unsqueeze(1).to_broadcast([P, P, PACK])
         z_last = []
@@ -233,5 +240,5 @@ def tile_picked_mcresid_none_p_kernel(
             z_last.append(z_grouped)
         for b in (2, 3):
             finish(
-                z_last[b - 2], b * P, (b + 1) * P, ("block%d" % b, "plane%d" % b), (nc.scalar.copy, nc.vector.tensor_copy)
+                z_last[b - 2], b * P, (b + 1) * P, ("block%d" % b, "plane%d" % b), (nc.scalar.copy, nc.vector.tensor_copy), 1
             )

@@ -177,17 +177,17 @@ def tile_picked_mcresid_none_p_kernel(
 
         out_rows = out.rearrange("(b p) j -> p b j", p=P)
 
-        def finish(z_grouped, lo, hi, tags, copies, stores):
-            z_q = quantise("z%d" % lo, z_grouped[:].rearrange("p j t -> p (j t)"), hi - lo, keep)
-            staged = keep.tile([P, PACK, hi - lo], F32, name="staged%d" % lo)
-            for g in range(2):
-                bank = psum.tile([P, 2, hi - lo], F32, name="out_bank%d_%d" % (lo, g), tag=tags[g])
-                for i in range(2):
-                    product(bank[:, i, :], w3_q, 2 * g + i, z_q, 0, hi - lo)
-                copies[g](staged[:, 2 * g : 2 * g + 2, :], bank[:])
-            for g in range(stores):
-                rows = slice(g * PACK // stores, (g + 1) * PACK // stores)
-                nc.sync.dma_start(out_rows[:, rows, lo:hi], staged[:, rows, :])
+        def finish(z_grouped, lo, tags, copies):
+            z_q = quantise("z%d" % lo, z_grouped[:].rearrange("p j t -> p (j t)"), HALF, keep)
+            staged = keep.tile([P, PACK, HALF], F32, name="staged%d" % lo)
+            per_bank = PACK // len(tags)
+            for g, tag in enumerate(tags):
+                rows = slice(g * per_bank, (g + 1) * per_bank)
+                bank = psum.tile([P, per_bank, HALF], F32, name="out_bank%d_%d" % (lo, g), tag=tag)
+                for i in range(per_bank):
+                    product(bank[:, i, :], w3_q, g * per_bank + i, z_q, 0, HALF)
+                copies[g % len(copies)](staged[:, rows, :], bank[:])
+                nc.sync.dma_start(out_rows[:, rows, lo : lo + HALF], staged[:, rows, :])
 
         planes = tuple(range(PACK))
         predict(0, 0, planes, term_tile(4, "first"), False)
@@ -230,15 +230,12 @@ def tile_picked_mcresid_none_p_kernel(
             for t in range(PACK):
                 nc.tensor.transpose(bank[:, t, :], clipped[:, t, :], identity[:])
             backs.append(bank)
-        finish(z_first, 0, HALF, ("plane0", "plane1"), (nc.scalar.copy, nc.scalar.copy), 2)
+        finish(z_first, 0, ("plane0", "plane1"), (nc.scalar.copy,))
 
         gain_wide = gain[:].unsqueeze(1).to_broadcast([P, P, PACK])
-        z_last = []
-        for b in (2, 3):
-            z_grouped = keep.tile([P, P, PACK], BF16, name="z_grouped%d" % b, tag="z_first" if b == 2 else "z_last", align_bytes=64)
-            nc.vector.tensor_tensor(z_grouped[:], backs[b - 2][:].rearrange("p t j -> p j t"), gain_wide, ALU.mult)
-            z_last.append(z_grouped)
-        for b in (2, 3):
-            finish(
-                z_last[b - 2], b * P, (b + 1) * P, ("block%d" % b, "plane%d" % b), (nc.scalar.copy, nc.vector.tensor_copy), 1
+        z_last = keep.tile([P, HALF, PACK], BF16, name="z_last", tag="z_first", align_bytes=64)
+        for i in range(2):
+            nc.vector.tensor_tensor(
+                z_last[:, i * P : (i + 1) * P, :], backs[i][:].rearrange("p t j -> p j t"), gain_wide, ALU.mult
             )
+        finish(z_last, HALF, ("block2", "block3", "plane2", "plane3"), (nc.vector.tensor_copy, nc.scalar.copy))

from contextlib import ExitStack

import concourse.mybir as mybir
from concourse.masks import make_identity

F32 = mybir.dt.float32
BF16 = mybir.dt.bfloat16
I32 = mybir.dt.int32
U32 = mybir.dt.uint32
U16 = mybir.dt.uint16
U8 = mybir.dt.uint8
FP8X4 = mybir.dt.float8_e4m3fn_x4
ALU = mybir.AluOpType
ACT = mybir.ActivationFunctionType

P = 128
PACK = 4
T, S, H, N = 2048, 512, 512, 512
CLIP = 1.5
FLOPS = 3 * 2 * 512 * 512 * 512
HALF = 256
BLOCKS = 4


def tile_picked_mcresid_none_p_kernel(
    tc, x_words, x_scales, w1, w2, a1, a2, gn, w3, offs, ref, c1, c2, out
):
    nc = tc.nc
    with ExitStack() as ctx:
        lists = ctx.enter_context(tc.tile_pool(name="lists", bufs=1))
        keep = ctx.enter_context(tc.tile_pool(name="keep", bufs=1))
        psum = ctx.enter_context(tc.psum_pool(name="psum", bufs=1))

        def load_list(name, src):
            tile = lists.tile([P, S // 16], U16, name=name)
            nc.sync.dma_start(tile[:], src)
            return tile

        def load_weight(name, src):
            raw = keep.tile([P, PACK, 512], F32, name=name)
            nc.sync.dma_start(raw[:], src.rearrange("(p j) c -> p j c", j=PACK))
            return raw

        def load_half(name, src, h):
            tile = keep.tile([P, PACK, HALF], F32, name=name, align_bytes=64)
            nc.sync.dma_start(tile[:], src.rearrange("(p t) c -> p t c", t=PACK)[:, :, h * HALF : (h + 1) * HALF])
            return tile

        x_bytes = keep.tile([P, T], U8, name="x_bytes", align_bytes=64)
        nc.vector.memset(x_bytes[:].bitcast(I32), 0)
        ref_list = load_list("ref_list", ref)
        w2_view = w2.rearrange("(p j) c -> p j c", j=PACK)
        w2_halves = [keep.tile([P, PACK, 256], F32, name="w2_raw%d" % h) for h in range(2)]
        nc.sync.dma_start(w2_halves[0][:], w2_view[:, :, 0:256])
        for r in range(4):
            nc.sync.dma_start(
                x_bytes[r:P:32, :].bitcast(I32),
                x_scales[0].rearrange("(q r) c -> r q c", r=4)[r].bitcast(I32),
            )
        offs_list = load_list("offs_list", offs)
        nc.sync.dma_start(w2_halves[1][:], w2_view[:, :, 256:512])
        x_packed = keep.tile([P, T], I32, name="x_packed", align_bytes=64)
        nc.sync.dma_start(x_packed[:], x_words[0].rearrange("p c r -> p (c r)").bitcast(I32))
        gain = keep.tile([P, PACK], F32, name="gain")
        nc.sync.dma_start(gain[:], gn.rearrange("(p t) o -> p (t o)", t=PACK))
        c1_list = load_list("c1_list", c1)
        c2_list = load_list("c2_list", c2)
        a_half = {}
        a_half[0, 0] = load_half("a1_0", a1, 0)
        w1_raw = load_weight("w1_raw", w1)
        a_half[1, 0] = load_half("a2_0", a2, 0)
        w3_halves = [load_half("w3_0", w3, 0)]
        a_half[0, 1] = load_half("a1_1", a1, 1)
        a_half[1, 1] = load_half("a2_1", a2, 1)
        w3_halves.append(load_half("w3_1", w3, 1))

        def gather_bytes(name, picks):
            tile = keep.tile([P, S], U8, name=name, align_bytes=64)
            nc.vector.tensor_copy(tile[:], x_bytes[:].indirect(picks[:]))
            return tile

        def gather_words(name, picks, parts):
            tile = keep.tile([P, S], U32, name=name, align_bytes=64)
            width = S // parts
            for i in range(parts):
                entries = picks[:, i * width // 16 : (i + 1) * width // 16]
                nc.vector.tensor_copy(tile[:, i * width : (i + 1) * width], x_packed[:].bitcast(U32).indirect(entries))
            return tile

        def round_dealt(name, raw, copy):
            grouped = keep.tile([P, 512 * PACK], BF16, name=name, align_bytes=64)
            copy(
                grouped[:].rearrange("p (t m j) -> p m j t", t=PACK, j=PACK),
                raw[:].rearrange("p j (m t) -> p m j t", t=PACK),
            )
            return grouped

        def round_plain(grouped, raw):
            nc.scalar.copy(
                grouped.rearrange("p (c i j) -> p c j i", i=4, j=PACK),
                raw[:].rearrange("p j (c i) -> p c j i", i=4),
            )

        def quantise(name, grouped, width, pool, tag=None):
            codes = pool.tile([P, width], U32, name=name + "_codes", tag=tag or name + "_codes", align_bytes=64)
            scales = pool.tile([P, width], U8, name=name + "_scales", align_bytes=64)
            nc.vector.quantize_mx(out=codes[:].bitcast(FP8X4), scales=scales[:], in_=grouped)
            return codes, scales

        def product(bank, stationary, block, moving, lo, hi):
            cols = slice(block * P, (block + 1) * P)
            nc.tensor.matmul_mx(
                out=bank,
                lhsT=stationary[0][:, cols].bitcast(FP8X4),
                lhsT_scale=stationary[1][:, cols],
                rhs=moving[0][:, lo:hi].bitcast(FP8X4),
                rhs_scale=moving[1][:, lo:hi],
                start=True,
                stop=True,
            )

        ref_bytes = gather_bytes("ref_bytes", ref_list)
        offs_bytes = gather_bytes("offs_bytes", offs_list)
        w2_grouped = keep.tile([P, 512 * PACK], BF16, name="w2_grouped", align_bytes=64)
        for h in range(2):
            nc.scalar.copy(
                w2_grouped[:].rearrange("p (t m j) -> p m j t", t=PACK, j=PACK)[:, 64 * h : 64 * (h + 1)],
                w2_halves[h][:].rearrange("p j (m t) -> p m j t", t=PACK),
            )
        w2_q = quantise("w2", w2_grouped[:], 512, keep)
        ref_words = gather_words("ref_words", ref_list, 2)
        offs_words = gather_words("offs_words", offs_list, 1)

        identity = keep.tile([P, P], F32, name="identity")
        make_identity(nc, identity[:])

        e_rows = []
        for t in range(PACK):
            row = keep.tile([P, S], F32, name="e_row%d" % t, align_bytes=64)
            spans = ((0, HALF, "block0"), (HALF, S, "plane0")) if t == 0 else ((0, S, "plane%d" % t),)
            for lo, hi, tag in spans:
                bank = psum.tile([P, hi - lo], F32, name="e_bank%d_%d" % (t, lo), tag=tag)
                product(bank[:], w2_q, t, (ref_words, ref_bytes), lo, hi)
                nc.scalar.activation(row[:, lo:hi], bank[:], ACT.Copy, scale=-1.0)
            e_rows.append(row)

        w1_grouped = round_dealt("w1_grouped", w1_raw, nc.scalar.copy)
        w3_grouped = keep.tile([P, 512 * PACK], BF16, name="w3_grouped", align_bytes=64)
        round_plain(w3_grouped[:, 0 : HALF * PACK], w3_halves[0])

        sums = [psum.tile([P, PACK, P], F32, name="sums%d" % b, tag="block%d" % b) for b in range(BLOCKS)]

        def add_turned(src, t, b, start, stop):
            nc.tensor.matmul(sums[b][:, t, :], lhsT=src, rhs=identity[:], start=start, stop=stop, is_transpose=True)

        def term_tile(count, tag):
            return keep.tile([P, count, HALF], F32, name="terms_" + tag, tag=tag, align_bytes=64)

        def predict(side, h, planes, terms, closes):
            picks = (c1_list, c2_list)[side]
            for n, t in enumerate(planes):
                nc.vector.tensor_tensor(
                    terms[:, n, :],
                    e_rows[t][:].indirect(picks[:, h * HALF // 16 : (h + 1) * HALF // 16]),
                    a_half[side, h][:, t, :],
                    ALU.mult,
                )
                for i in range(2):
                    add_turned(
                        terms[:, n, i * P : (i + 1) * P], t, 2 * h + i, t == 0 and side == 0 and h == 0, closes and t == PACK - 1
                    )

        def clip(b):
            clipped = keep.tile([P, PACK, P], F32, name="clipped%d" % b)
            nc.vector.tensor_scalar(clipped[:], sums[b][:], -CLIP, CLIP, ALU.max, ALU.min)
            return clipped

        out_rows = out.rearrange("(b p) j -> p b j", p=P)

        def finish(z_grouped, lo, tags, copies):
            z_q = quantise("z%d" % lo, z_grouped[:].rearrange("p j t -> p (j t)"), HALF, keep)
            staged = keep.tile([P, PACK, HALF], F32, name="staged%d" % lo)
            per_bank = PACK // len(tags)
            for g, tag in enumerate(tags):
                rows = slice(g * per_bank, (g + 1) * per_bank)
                bank = psum.tile([P, per_bank, HALF], F32, name="out_bank%d_%d" % (lo, g), tag=tag)
                for i in range(per_bank):
                    product(bank[:, i, :], w3_q, g * per_bank + i, z_q, 0, HALF)
                copies[g % len(copies)](staged[:, rows, :], bank[:])
                nc.sync.dma_start(out_rows[:, rows, lo : lo + HALF], staged[:, rows, :])

        planes = tuple(range(PACK))
        predict(0, 0, planes, term_tile(4, "first"), False)
        predict(1, 0, planes[:3], term_tile(3, "second"), False)
        w1_q = quantise("w1", w1_grouped[:], 512, keep)
        y_banks = []
        for t in range(PACK):
            bank = psum.tile([P, S], F32, name="y_bank%d" % t, tag="plane%d" % t)
            product(bank[:], w1_q, t, (offs_words, offs_bytes), 0, S)
            y_banks.append(bank)
        after_w1 = term_tile(5, "w1_grouped")
        predict(1, 0, planes[3:], after_w1[:, 0:1, :], False)
        for h in range(2):
            y_half = keep.tile([P, PACK, HALF], F32, name="y_half%d" % h, tag=("w3_0", "y_last")[h], align_bytes=64)
            for t in range(PACK):
                nc.scalar.copy(y_half[:, t, :], y_banks[t][:, h * HALF : (h + 1) * HALF])
                for i in range(2):
                    add_turned(y_half[:, t, i * P : (i + 1) * P], t, 2 * h + i, h == 1 and t == 0, h == 0 and t == PACK - 1)
        round_plain(w3_grouped[:, HALF * PACK :], w3_halves[1])
        predict(0, 1, planes, after_w1[:, 1:5, :], False)

        first = [clip(b) for b in range(2)]
        z_planes = keep.tile([P, PACK, HALF], BF16, name="z_planes", align_bytes=64)
        for t in range(PACK):
            bank = psum.tile([P, HALF], F32, name="back_plane%d" % t, tag="plane%d" % t)
            for b in range(2):
                nc.tensor.transpose(bank[:, b * P : (b + 1) * P], first[b][:, t, :], identity[:])
            nc.scalar.activation(z_planes[:, t, :], bank[:], ACT.Copy, scale=gain[:, t : t + 1])
        z_first = keep.tile([P, HALF, PACK], BF16, name="z_first", align_bytes=64)
        nc.scalar.copy(
            z_first[:].rearrange("p (c i) t -> p c t i", i=4), z_planes[:].rearrange("p t (c i) -> p c t i", i=4)
        )

        predict(1, 1, planes, term_tile(4, "w3_0"), True)
        w3_q = quantise("w3", w3_grouped[:], 512, keep, "e_row3")
        backs = []
        for b in (2, 3):
            clipped = clip(b)
            bank = psum.tile([P, PACK, P], F32, name="back_block%d" % b, tag="block%d" % (b - 2))
            for t in range(PACK):
                nc.tensor.transpose(bank[:, t, :], clipped[:, t, :], identity[:])
            backs.append(bank)
        finish(z_first, 0, ("plane0", "plane1"), (nc.scalar.copy,))

        gain_wide = gain[:].unsqueeze(1).to_broadcast([P, P, PACK])
        z_last = keep.tile([P, HALF, PACK], BF16, name="z_last", tag="z_first", align_bytes=64)
        for i in range(2):
            nc.vector.tensor_tensor(
                z_last[:, i * P : (i + 1) * P, :], backs[i][:].rearrange("p t j -> p j t"), gain_wide, ALU.mult
            )
        finish(z_last, HALF, ("block2", "block3", "plane2", "plane3"), (nc.vector.tensor_copy, nc.scalar.copy))
